import numpy as np
import ml_dtypes


def mxq(x, axis, fmt="e4m3"):
    dtype, down = {"e4m3": (ml_dtypes.float8_e4m3fn, 7), "e5m2": (ml_dtypes.float8_e5m2, 14)}[fmt]
    v = np.moveaxis(np.asarray(x, np.float32).astype(ml_dtypes.bfloat16).astype(np.float64), axis, -1)
    blocks = v.reshape(v.shape[:-1] + (-1, 32))
    amax = np.abs(blocks).max(-1, keepdims=True)
    byte = np.maximum(np.where(amax > 0, np.frexp(amax)[1] - 1 + 127, 0) - down, 1)
    scale = np.exp2(byte - 127.0)
    codes = (blocks / scale).astype(np.float32).astype(dtype).astype(np.float64)
    return np.moveaxis((codes * scale).reshape(v.shape), -1, axis)


WIDE = False


def mx_kscale(k):
    if not WIDE:
        return np.ones(k)
    levels = np.array([10, -10, 5, -5, 0])
    if k % 512:
        return np.exp2(np.random.permutation(np.resize(levels, k // 32))).repeat(32)
    a = np.empty((k // 512, 16))
    for p in range(k // 512):
        a[p, :8] = np.random.permutation(np.resize(levels, 8))
        for g in range(8):
            far = levels[np.abs(levels - a[p, g]) >= 10]
            a[p, g + 8] = far[np.random.randint(len(far))]
    return np.exp2(a.ravel()).repeat(32)


def f64(x):
    return np.asarray(x).astype(np.float64)


E2M1 = np.array([0.0, 0.5, 1.0, 1.5, 2.0, 3.0, 4.0, 6.0, -0.0, -0.5, -1.0, -1.5, -2.0, -3.0, -4.0, -6.0])


def pack_weight(w, fmt):
    k, n = w.shape
    w = f64(np.asarray(w, np.float32).astype(ml_dtypes.bfloat16)).reshape(k // 32, 32, n)
    amax = np.abs(w).max(1)
    if fmt == "e4m3":
        byte = np.frexp(amax)[1] - 1 + 127 - 7
    else:
        mant, ex = np.frexp(amax / 6.0)
        byte = np.where(mant > 0.5, ex, ex - 1) + 127
    byte = np.clip(np.where(amax > 0, byte, 1), 1, 254)
    scaled = (w * np.exp2(127.0 - byte)[:, None, :]).reshape(k, n).astype(np.float32)
    by_word = np.ascontiguousarray(scaled.reshape(k // 512, 128, 4, n).transpose(0, 1, 3, 2))
    if fmt == "e4m3":
        words = by_word.astype(ml_dtypes.float8_e4m3fn).view(np.uint8)
    else:
        c = by_word.astype(ml_dtypes.float4_e2m1fn).view(np.uint8) & 0xF
        words = (c[..., 0::2] | (c[..., 1::2] << 4)).reshape(k // 512, 128, 2 * n)
    return np.ascontiguousarray(words), np.ascontiguousarray(byte.astype(np.uint8).reshape(k // 512, 16, n))


def unpack_weight(words, scales, fmt):
    g, _, n = scales.shape
    words = np.ascontiguousarray(words).reshape(g, 128, n, -1)
    if fmt == "e4m3":
        vals = words.view(ml_dtypes.float8_e4m3fn).astype(np.float64)
    else:
        nib = np.empty((g, 128, n, 4), np.uint8)
        nib[..., 0::2] = words & 0xF
        nib[..., 1::2] = words >> 4
        vals = E2M1[nib]
    vals = vals * np.repeat(np.exp2(scales.astype(np.float64) - 127.0), 8, axis=1)[..., None]
    return vals.transpose(0, 1, 3, 2).reshape(g * 512, n)


def bf(x):
    return np.asarray(x, np.float32).astype(ml_dtypes.bfloat16)


def planes(Y):
    r, m = Y.shape
    b = f64(bf(Y)).reshape(r // 32, 32, m)
    amax = np.abs(b).max(1)
    byte = np.clip(np.where(amax > 0, np.frexp(amax)[1] - 1 + 127 - 7, 1), 1, 254)
    codes = (b * np.exp2(127.0 - byte)[:, None, :]).reshape(r, m).astype(np.float32).astype(ml_dtypes.float8_e4m3fn).view(np.uint8)
    words = codes.reshape(r // 512, 128, 4, m).transpose(0, 1, 3, 2)
    return np.ascontiguousarray(words), np.ascontiguousarray(byte.astype(np.uint8).reshape(r // 512, 16, m))


K, L, T, R, N = 1024, 512, 512, 512, 512


def setup_inputs():
    n = np.random.standard_normal
    fk = mx_kscale(K)
    fr = mx_kscale(R)
    fl = mx_kscale(L)
    xtp = pack_weight(n((K, T)) / fk[:, None], "e2m1")
    wap = pack_weight(n((K, R)) * 1 / np.sqrt(K) * fk[:, None] * fr, "e4m3")
    xqp = pack_weight(n((L, T)) / fl[:, None], "e2m1")
    wcp = pack_weight(n((L, R)) * 1 / np.sqrt(L) * fl[:, None] * fr, "e4m3")
    wbp = pack_weight(n((R, N)) * 1 / np.sqrt(R) / fr[:, None], "e2m1")
    return {
        "xt_words": xtp[0],
        "xt_scales": xtp[1],
        "wa_words": wap[0],
        "wa_scales": wap[1],
        "xq_words": xqp[0],
        "xq_scales": xqp[1],
        "wc_words": wcp[0],
        "wc_scales": wcp[1],
        "wb_words": wbp[0],
        "wb_scales": wbp[1],
        "b": (np.random.uniform(-0.5, 0.5, (N, 1))).astype(np.float32),
    }


def reference(xt_words, xt_scales, wa_words, wa_scales, xq_words, xq_scales, wc_words, wc_scales, wb_words, wb_scales, b):
    xtu = unpack_weight(xt_words, xt_scales, "e2m1")
    wau = unpack_weight(wa_words, wa_scales, "e4m3")
    xqu = unpack_weight(xq_words, xq_scales, "e2m1")
    wcu = unpack_weight(wc_words, wc_scales, "e4m3")
    wbu = unpack_weight(wb_words, wb_scales, "e2m1")
    z = wau.T @ xtu + wcu.T @ xqu
    z1 = np.pad(z, ((0, 0), (1, 0)))[:, :T]
    z2 = np.pad(z, ((0, 0), (2, 0)))[:, :T]
    hid = np.maximum(z + 0.5 * z1 + 0.25 * z2, 0.0)
    hidq = mxq(hid, 0, "e4m3")
    p = wbu.T @ hidq
    y = p + f64(b)
    words, scales = planes(y)
    return y, words, scales

@@ -1,0 +1,210 @@
+from contextlib import ExitStack
+
+import concourse.mybir as mybir
+
+K, L, T, R, N = 1024, 512, 512, 512, 512
+FLOPS = 2 * (K + L) * R * T + 2 * R * N * T
+
+F32 = mybir.dt.float32
+BF16 = mybir.dt.bfloat16
+I32 = mybir.dt.int32
+U8 = mybir.dt.uint8
+FP8X4 = mybir.dt.float8_e4m3fn_x4
+FP4X4 = mybir.dt.float4_e2m1fn_x4
+ALU = mybir.AluOpType
+ACT = mybir.ActivationFunctionType
+
+P = 128
+PACK = 4
+CHUNK = 128
+CHUNKS = T // CHUNK
+WIDE = CHUNK * PACK
+HALO = 2 * PACK
+
+
+def tile_mix_momentum_of_two_inputs_pl_kernel(
+    tc, xt_words, xt_scales, wa_words, wa_scales, xq_words, xq_scales, wc_words, wc_scales, wb_words, wb_scales, b,
+    out_0, out_1, out_2,
+):
+    nc = tc.nc
+    with ExitStack() as ctx:
+        sb = ctx.enter_context(tc.tile_pool(name="sb", bufs=1))
+        ps = ctx.enter_context(tc.psum_pool(name="ps", bufs=1))
+        ctx.enter_context(tc.manual_schedule())
+
+        def tiles(pool, name, count, shape, dtype):
+            return [pool.tile(shape, dtype, name="%s%d" % (name, i), align_bytes=64) for i in range(count)]
+
+        xt_sb = sb.tile([P, 2, 2 * T], U8, align_bytes=64)
+        xq_sb = sb.tile([P, 2 * T], U8, align_bytes=64)
+        wa_raw = sb.tile([P, 2, R], I32, align_bytes=64)
+        wc_raw = sb.tile([P, R], I32, align_bytes=64)
+        planes = sb.tile([P, 7 * T], U8, align_bytes=64)
+        x_words = [xt_sb[:, 0, :], xt_sb[:, 1, :], xq_sb[:]]
+        w_raw = [wa_raw[:, 0, :], wa_raw[:, 1, :], wc_raw[:]]
+        w_plane_raw = [planes[:, 0:T], planes[:, T : 2 * T], planes[:, 4 * T : 5 * T]]
+        x_plane = [planes[:, 2 * T : 3 * T], planes[:, 3 * T : 4 * T], planes[:, 5 * T : 6 * T]]
+        wb_plane_raw = planes[:, 6 * T : 7 * T]
+        w_words = tiles(sb, "w_words", 3, [P, R], I32)
+        w_plane = tiles(sb, "w_plane", 3, [P, R], U8)
+        wb_raw = sb.tile([P, 2 * N], U8, align_bytes=64)
+        wb_dealt = sb.tile([P, 2 * N], U8, align_bytes=64)
+        wb_plane = sb.tile([P, N], U8, align_bytes=64)
+        bias = sb.tile([P, PACK], F32, align_bytes=64)
+        warm = sb.tile([P, 1], F32, align_bytes=64)
+        z = sb.tile([P, HALO + PACK * T], F32, align_bytes=64)
+        part = tiles(sb, "part", CHUNKS, [P, WIDE], F32)
+        pre = tiles(sb, "pre", CHUNKS, [P, WIDE], BF16)
+        hid = tiles(sb, "hid", CHUNKS, [P, WIDE], BF16)
+        hid_words = tiles(sb, "hid_words", CHUNKS, [P, CHUNK], I32)
+        hid_plane = tiles(sb, "hid_plane", CHUNKS, [P, CHUNK], U8)
+        y = tiles(sb, "y", CHUNKS, [P, PACK, CHUNK], F32)
+        y_bf = tiles(sb, "y_bf", CHUNKS, [P, WIDE], BF16)
+        y_words = tiles(sb, "y_words", CHUNKS, [P, CHUNK], I32)
+        y_plane = sb.tile([P, T], U8, align_bytes=64)
+        z_ps = [ps.tile([P, PACK, CHUNK], F32, name="z_ps%d" % c) for c in range(CHUNKS)]
+        p_ps = [ps.tile([P, PACK, CHUNK], F32, name="p_ps%d" % c) for c in range(CHUNKS)]
+
+        def load_scales(queue, first, scales, q):
+            passes = scales.shape[0]
+            dst = planes[32 * q : 32 * q + 4, T * first : T * (first + passes)].bitcast(I32)
+            queue.dma_start(
+                out=dst.rearrange("r (g c) -> r g c", g=passes),
+                in_=scales[:, 4 * q : 4 * q + 4, :].bitcast(I32).rearrange("g r c -> r g c"),
+            )
+
+        nc.vector.memset(planes[:, 0 : 4 * T].bitcast(I32), 0)
+        nc.vector.memset(planes[:, 4 * T : 7 * T].bitcast(I32), 0)
+        nc.vector.memset(z[:, 0:HALO], 0.0)
+
+        nc.sync.dma_start(out=xt_sb[:].bitcast(I32), in_=xt_words.bitcast(I32).rearrange("g p c -> p g c"))
+        nc.sync.dma_start(out=wa_raw[:], in_=wa_words.rearrange("g p c t -> p g (c t)").bitcast(I32))
+        for q in range(4):
+            load_scales(nc.scalar, 0, wa_scales, q)
+        for q in range(2):
+            load_scales(nc.sync, 2, xt_scales, q)
+        for q in range(4):
+            load_scales(nc.gpsimd, 6, wb_scales, q)
+        nc.scalar.activation(out=warm[:], in_=z[:, 0:1], func=ACT.Identity)
+        nc.sync.dma_start(out=wc_raw[:], in_=wc_words[0].rearrange("p c t -> p (c t)").bitcast(I32))
+        nc.sync.dma_start(out=xq_sb[:].bitcast(I32), in_=xq_words[0].bitcast(I32))
+        for q in range(2, 4):
+            load_scales(nc.scalar, 2, xt_scales, q)
+        for q in range(4):
+            load_scales(nc.scalar, 4, wc_scales, q)
+        nc.sync.dma_start(out=wb_raw[:].bitcast(I32), in_=wb_words[0].bitcast(I32))
+        nc.sync.dma_start(out=bias[:], in_=b.rearrange("(p i) o -> p (i o)", i=PACK))
+        for q in range(4):
+            load_scales(nc.scalar, 5, xq_scales, q)
+
+        def deal_plane(dst, src):
+            nc.vector.tensor_copy(
+                out=dst[:].rearrange("p (j h l) -> p h j l", j=PACK, l=16),
+                in_=src.rearrange("p (h l j) -> p h j l", j=PACK, l=16),
+            )
+
+        for g in range(3):
+            deal_plane(w_plane[g], w_plane_raw[g])
+            nc.vector.tensor_copy(
+                out=w_words[g][:].rearrange("p (j h l) -> p h j l", j=PACK, l=4),
+                in_=w_raw[g].rearrange("p (h l j) -> p h j l", j=PACK, l=4),
+            )
+        deal_plane(wb_plane, wb_plane_raw)
+        nc.vector.tensor_copy(
+            out=wb_dealt[:].rearrange("p (j h l e) -> p h j l e", j=PACK, l=8, e=2),
+            in_=wb_raw[:].rearrange("p (h l j e) -> p h j l e", j=PACK, l=8, e=2),
+        )
+
+        def first_layer(c, g):
+            for j in range(PACK):
+                nc.tensor.matmul_mx(
+                    out=z_ps[c][:, j, :],
+                    lhsT=w_words[g][:, P * j : P * (j + 1)].bitcast(FP8X4),
+                    lhsT_scale=w_plane[g][:, P * j : P * (j + 1)],
+                    rhs=x_words[g][:, 2 * CHUNK * c : 2 * CHUNK * (c + 1)].bitcast(FP4X4),
+                    rhs_scale=x_plane[g][:, CHUNK * c : CHUNK * (c + 1)],
+                    start=(g == 0 and j == 0),
+                    stop=(g == 2 and j == PACK - 1),
+                )
+
+        for g in range(3):
+            for c in range(CHUNKS):
+                first_layer(c, g)
+
+        for c in range(CHUNKS):
+            nc.scalar.copy(
+                out=z[:, HALO + WIDE * c : HALO + WIDE * (c + 1)].rearrange("p (t j) -> p t j", j=PACK),
+                in_=z_ps[c][:].rearrange("p j t -> p t j"),
+            )
+
+        def z_back(c, back):
+            first = HALO + WIDE * c - PACK * back
+            return z[:, first : first + WIDE]
+
+        def add_previous(c):
+            nc.vector.scalar_tensor_tensor(out=part[c][:], in0=z_back(c, 1), scalar=0.5, in1=z_back(c, 0), op0=ALU.mult, op1=ALU.add)
+
+        def add_second(c):
+            nc.vector.scalar_tensor_tensor(out=pre[c][:], in0=z_back(c, 2), scalar=0.25, in1=part[c][:], op0=ALU.mult, op1=ALU.add)
+
+        def relu(c):
+            nc.vector.tensor_scalar_max(out=hid[c][:], in0=pre[c][:], scalar1=0.0)
+
+        def quantise_hid(c):
+            nc.vector.quantize_mx(out=hid_words[c][:].bitcast(FP8X4), scales=hid_plane[c][:], in_=hid[c][:])
+
+        def second_layer(c):
+            for i in range(PACK):
+                nc.tensor.matmul_mx(
+                    out=p_ps[c][:, i, :],
+                    lhsT=wb_dealt[:, 2 * P * i : 2 * P * (i + 1)].bitcast(FP4X4),
+                    lhsT_scale=wb_plane[:, P * i : P * (i + 1)],
+                    rhs=hid_words[c][:].bitcast(FP8X4),
+                    rhs_scale=hid_plane[c][:],
+                    start=True,
+                    stop=True,
+                )
+            for i in range(PACK):
+                nc.scalar.activation(out=y[c][:, i, :], in_=p_ps[c][:, i, :], func=ACT.Identity, bias=bias[:, i : i + 1])
+            nc.sync.dma_start(
+                out=out_0.rearrange("(p i) t -> p i t", i=PACK)[:, :, CHUNK * c : CHUNK * (c + 1)], in_=y[c][:]
+            )
+
+        def round_y(c):
+            nc.vector.tensor_copy(
+                out=y_bf[c][:].rearrange("p (h l i) -> p h i l", i=PACK, l=4),
+                in_=y[c][:].rearrange("p i (h l) -> p h i l", l=4),
+            )
+
+        def quantise_y(c):
+            nc.vector.quantize_mx(
+                out=y_words[c][:].bitcast(FP8X4), scales=y_plane[:, CHUNK * c : CHUNK * (c + 1)], in_=y_bf[c][:]
+            )
+            nc.sync.dma_start(
+                out=out_1[0].rearrange("p c t -> p (c t)").bitcast(I32)[:, CHUNK * c : CHUNK * (c + 1)], in_=y_words[c][:]
+            )
+
+        add_previous(0)
+        add_second(0)
+        for c in range(1, CHUNKS):
+            add_previous(c)
+            relu(c - 1)
+            add_second(c)
+            quantise_hid(c - 1)
+            second_layer(c - 1)
+        round_y(0)
+        relu(CHUNKS - 1)
+        quantise_y(0)
+        quantise_hid(CHUNKS - 1)
+        second_layer(CHUNKS - 1)
+        round_y(1)
+        round_y(2)
+        quantise_y(1)
+        quantise_y(2)
+        round_y(3)
+        quantise_y(3)
+        for q in range(4):
+            queue = nc.sync if q % 2 else nc.scalar
+            queue.dma_start(
+                out=out_2[0, 4 * q : 4 * q + 4, :].bitcast(I32), in_=y_plane[32 * q : 32 * q + 4, :].bitcast(I32)
+            )

@@ -60,7 +60,7 @@ def tile_mix_momentum_of_two_inputs_pl_kernel(
         hid_plane = tiles(sb, "hid_plane", CHUNKS, [P, CHUNK], U8)
         y = tiles(sb, "y", CHUNKS, [P, PACK, CHUNK], F32)
         y_bf = tiles(sb, "y_bf", CHUNKS, [P, WIDE], BF16)
-        y_words = tiles(sb, "y_words", CHUNKS, [P, CHUNK], I32)
+        y_words = sb.tile([P, T], I32, align_bytes=64)
         y_plane = sb.tile([P, T], U8, align_bytes=64)
         z_ps = [ps.tile([P, PACK, CHUNK], F32, name="z_ps%d" % c) for c in range(CHUNKS)]
         p_ps = [ps.tile([P, PACK, CHUNK], F32, name="p_ps%d" % c) for c in range(CHUNKS)]
@@ -73,29 +73,29 @@ def tile_mix_momentum_of_two_inputs_pl_kernel(
                 in_=scales[:, 4 * q : 4 * q + 4, :].bitcast(I32).rearrange("g r c -> r g c"),
             )
 
-        nc.vector.memset(planes[:, 0 : 4 * T].bitcast(I32), 0)
-        nc.vector.memset(planes[:, 4 * T : 7 * T].bitcast(I32), 0)
+        nc.vector.memset(planes[:, 0 : 2 * T].bitcast(I32), 0)
+        nc.vector.memset(planes[:, 2 * T : 7 * T].bitcast(I32), 0)
         nc.vector.memset(z[:, 0:HALO], 0.0)
+        nc.scalar.activation(out=warm[:], in_=z[:, 0:1], func=ACT.Identity)
 
         nc.sync.dma_start(out=xt_sb[:].bitcast(I32), in_=xt_words.bitcast(I32).rearrange("g p c -> p g c"))
-        nc.sync.dma_start(out=wa_raw[:], in_=wa_words.rearrange("g p c t -> p g (c t)").bitcast(I32))
         for q in range(4):
-            load_scales(nc.scalar, 0, wa_scales, q)
+            load_scales(nc.sync, 0, wa_scales, q)
         for q in range(2):
             load_scales(nc.sync, 2, xt_scales, q)
-        for q in range(4):
-            load_scales(nc.gpsimd, 6, wb_scales, q)
-        nc.scalar.activation(out=warm[:], in_=z[:, 0:1], func=ACT.Identity)
-        nc.sync.dma_start(out=wc_raw[:], in_=wc_words[0].rearrange("p c t -> p (c t)").bitcast(I32))
-        nc.sync.dma_start(out=xq_sb[:].bitcast(I32), in_=xq_words[0].bitcast(I32))
+        nc.sync.dma_start(out=wa_raw[:], in_=wa_words.rearrange("g p c t -> p g (c t)").bitcast(I32))
         for q in range(2, 4):
-            load_scales(nc.scalar, 2, xt_scales, q)
+            load_scales(nc.sync, 2, xt_scales, q)
+        nc.sync.dma_start(out=wc_raw[:], in_=wc_words[0].rearrange("p c t -> p (c t)").bitcast(I32))
         for q in range(4):
-            load_scales(nc.scalar, 4, wc_scales, q)
+            load_scales(nc.sync, 4, wc_scales, q)
+        nc.sync.dma_start(out=xq_sb[:].bitcast(I32), in_=xq_words[0].bitcast(I32))
+        for q in range(4):
+            load_scales(nc.sync, 5, xq_scales, q)
         nc.sync.dma_start(out=wb_raw[:].bitcast(I32), in_=wb_words[0].bitcast(I32))
-        nc.sync.dma_start(out=bias[:], in_=b.rearrange("(p i) o -> p (i o)", i=PACK))
         for q in range(4):
-            load_scales(nc.scalar, 5, xq_scales, q)
+            load_scales(nc.sync, 6, wb_scales, q)
+        nc.sync.dma_start(out=bias[:], in_=b.rearrange("(p i) o -> p (i o)", i=PACK))
 
         def deal_plane(dst, src):
             nc.vector.tensor_copy(
@@ -103,13 +103,18 @@ def tile_mix_momentum_of_two_inputs_pl_kernel(
                 in_=src.rearrange("p (h l j) -> p h j l", j=PACK, l=16),
             )
 
-        for g in range(3):
-            deal_plane(w_plane[g], w_plane_raw[g])
+        def deal_words(g):
             nc.vector.tensor_copy(
                 out=w_words[g][:].rearrange("p (j h l) -> p h j l", j=PACK, l=4),
                 in_=w_raw[g].rearrange("p (h l j) -> p h j l", j=PACK, l=4),
             )
-        deal_plane(wb_plane, wb_plane_raw)
+
+        deal_plane(w_plane[0], w_plane_raw[0])
+        deal_plane(w_plane[1], w_plane_raw[1])
+        deal_words(0)
+        deal_words(1)
+        deal_words(2)
+        deal_plane(w_plane[2], w_plane_raw[2])
         nc.vector.tensor_copy(
             out=wb_dealt[:].rearrange("p (j h l e) -> p h j l e", j=PACK, l=8, e=2),
             in_=wb_raw[:].rearrange("p (h l j e) -> p h j l e", j=PACK, l=8, e=2),
@@ -127,36 +132,53 @@ def tile_mix_momentum_of_two_inputs_pl_kernel(
                     stop=(g == 2 and j == PACK - 1),
                 )
 
-        for g in range(3):
-            for c in range(CHUNKS):
+        for c, g in [(0, 0), (0, 1), (1, 0), (0, 2), (1, 1), (1, 2)]:
+            first_layer(c, g)
+        for c in range(2, CHUNKS):
+            for g in range(3):
                 first_layer(c, g)
 
-        for c in range(CHUNKS):
+        def copy_z(c, lo=0, hi=CHUNK):
+            first = HALO + WIDE * c
             nc.scalar.copy(
-                out=z[:, HALO + WIDE * c : HALO + WIDE * (c + 1)].rearrange("p (t j) -> p t j", j=PACK),
-                in_=z_ps[c][:].rearrange("p j t -> p t j"),
+                out=z[:, first + PACK * lo : first + PACK * hi].rearrange("p (t j) -> p t j", j=PACK),
+                in_=z_ps[c][:, :, lo:hi].rearrange("p j t -> p t j"),
             )
 
-        def z_back(c, back):
+        copy_z(0, 0, CHUNK // 2)
+        copy_z(0, CHUNK // 2, CHUNK)
+        for c in range(1, CHUNKS):
+            copy_z(c)
+
+        def z_back(c, back, lo, hi):
             first = HALO + WIDE * c - PACK * back
-            return z[:, first : first + WIDE]
+            return z[:, first + PACK * lo : first + PACK * hi]
 
-        def add_previous(c):
-            nc.vector.scalar_tensor_tensor(out=part[c][:], in0=z_back(c, 1), scalar=0.5, in1=z_back(c, 0), op0=ALU.mult, op1=ALU.add)
+        def add_previous(c, lo=0, hi=CHUNK):
+            nc.vector.scalar_tensor_tensor(
+                out=part[c][:, PACK * lo : PACK * hi], in0=z_back(c, 1, lo, hi), scalar=0.5, in1=z_back(c, 0, lo, hi),
+                op0=ALU.mult, op1=ALU.add,
+            )
 
-        def add_second(c):
-            nc.vector.scalar_tensor_tensor(out=pre[c][:], in0=z_back(c, 2), scalar=0.25, in1=part[c][:], op0=ALU.mult, op1=ALU.add)
+        def add_second(c, lo=0, hi=CHUNK):
+            nc.vector.scalar_tensor_tensor(
+                out=pre[c][:, PACK * lo : PACK * hi], in0=z_back(c, 2, lo, hi), scalar=0.25,
+                in1=part[c][:, PACK * lo : PACK * hi], op0=ALU.mult, op1=ALU.add,
+            )
 
-        def relu(c):
+        def relu_scalar(c):
+            nc.scalar.activation(out=hid[c][:], in_=pre[c][:], func=ACT.Relu)
+
+        def relu_vector(c):
             nc.vector.tensor_scalar_max(out=hid[c][:], in0=pre[c][:], scalar1=0.0)
 
         def quantise_hid(c):
             nc.vector.quantize_mx(out=hid_words[c][:].bitcast(FP8X4), scales=hid_plane[c][:], in_=hid[c][:])
 
-        def second_layer(c):
+        def second_layer(c, bank):
             for i in range(PACK):
                 nc.tensor.matmul_mx(
-                    out=p_ps[c][:, i, :],
+                    out=bank[:, i, :],
                     lhsT=wb_dealt[:, 2 * P * i : 2 * P * (i + 1)].bitcast(FP4X4),
                     lhsT_scale=wb_plane[:, P * i : P * (i + 1)],
                     rhs=hid_words[c][:].bitcast(FP8X4),
@@ -164,6 +186,8 @@ def tile_mix_momentum_of_two_inputs_pl_kernel(
                     start=True,
                     stop=True,
                 )
+
+        def store_y(c):
             for i in range(PACK):
                 nc.scalar.activation(out=y[c][:, i, :], in_=p_ps[c][:, i, :], func=ACT.Identity, bias=bias[:, i : i + 1])
             nc.sync.dma_start(
@@ -177,32 +201,56 @@ def tile_mix_momentum_of_two_inputs_pl_kernel(
             )
 
         def quantise_y(c):
-            nc.vector.quantize_mx(
-                out=y_words[c][:].bitcast(FP8X4), scales=y_plane[:, CHUNK * c : CHUNK * (c + 1)], in_=y_bf[c][:]
-            )
-            nc.sync.dma_start(
-                out=out_1[0].rearrange("p c t -> p (c t)").bitcast(I32)[:, CHUNK * c : CHUNK * (c + 1)], in_=y_words[c][:]
-            )
+            cols = slice(CHUNK * c, CHUNK * (c + 1))
+            nc.vector.quantize_mx(out=y_words[:, cols].bitcast(FP8X4), scales=y_plane[:, cols], in_=y_bf[c][:])
 
-        add_previous(0)
-        add_second(0)
-        for c in range(1, CHUNKS):
-            add_previous(c)
-            relu(c - 1)
-            add_second(c)
-            quantise_hid(c - 1)
-            second_layer(c - 1)
+        def store_words(first, last):
+            cols = slice(CHUNK * first, CHUNK * last)
+            nc.sync.dma_start(out=out_1[0].rearrange("p c t -> p (c t)").bitcast(I32)[:, cols], in_=y_words[:, cols])
+
+        add_previous(0, 0, CHUNK // 2)
+        add_previous(0, CHUNK // 2, CHUNK)
+        add_second(0, 0, CHUNK // 2)
+        add_second(0, CHUNK // 2, CHUNK)
+        relu_scalar(0)
+        add_previous(1)
+        add_previous(2)
+        add_second(1)
+        relu_scalar(1)
+        deal_plane(wb_plane, wb_plane_raw)
+        quantise_hid(0)
+        second_layer(0, p_ps[0])
+        add_second(2)
+        relu_scalar(2)
+        store_y(0)
+        add_previous(3)
+        quantise_hid(1)
+        second_layer(1, p_ps[1])
+        store_y(1)
+        add_second(3)
+        quantise_hid(2)
+        second_layer(2, p_ps[2])
+        store_y(2)
+        relu_vector(3)
         round_y(0)
-        relu(CHUNKS - 1)
+        quantise_hid(3)
+        second_layer(3, z_ps[0])
+        second_layer(3, p_ps[3])
+        store_y(3)
         quantise_y(0)
-        quantise_hid(CHUNKS - 1)
-        second_layer(CHUNKS - 1)
         round_y(1)
         round_y(2)
         quantise_y(1)
+        nc.vector.tensor_tensor(
+            out=y_bf[3][:].rearrange("p (t i) -> p t i", i=PACK),
+            in0=z_ps[0][:].rearrange("p i t -> p t i"),
+            in1=bias[:].unsqueeze(1).to_broadcast([P, CHUNK, PACK]),
+            op=ALU.add,
+        )
         quantise_y(2)
-        round_y(3)
+        store_words(0, 3)
         quantise_y(3)
+        store_words(3, 4)
         for q in range(4):
             queue = nc.sync if q % 2 else nc.scalar
             queue.dma_start(

@@ -78,19 +78,19 @@ def tile_mix_momentum_of_two_inputs_pl_kernel(
         nc.vector.memset(z[:, 0:HALO], 0.0)
         nc.scalar.activation(out=warm[:], in_=z[:, 0:1], func=ACT.Identity)
 
+        for q in range(2):
+            load_scales(nc.gpsimd, 5, xq_scales, q)
         nc.sync.dma_start(out=xt_sb[:].bitcast(I32), in_=xt_words.bitcast(I32).rearrange("g p c -> p g c"))
         for q in range(4):
             load_scales(nc.sync, 0, wa_scales, q)
-        for q in range(2):
-            load_scales(nc.sync, 2, xt_scales, q)
         nc.sync.dma_start(out=wa_raw[:], in_=wa_words.rearrange("g p c t -> p g (c t)").bitcast(I32))
-        for q in range(2, 4):
+        for q in range(4):
             load_scales(nc.sync, 2, xt_scales, q)
         nc.sync.dma_start(out=wc_raw[:], in_=wc_words[0].rearrange("p c t -> p (c t)").bitcast(I32))
-        for q in range(4):
-            load_scales(nc.sync, 4, wc_scales, q)
         nc.sync.dma_start(out=xq_sb[:].bitcast(I32), in_=xq_words[0].bitcast(I32))
         for q in range(4):
+            load_scales(nc.sync, 4, wc_scales, q)
+        for q in range(2, 4):
             load_scales(nc.sync, 5, xq_scales, q)
         nc.sync.dma_start(out=wb_raw[:].bitcast(I32), in_=wb_words[0].bitcast(I32))
         for q in range(4):
@@ -138,6 +138,20 @@ def tile_mix_momentum_of_two_inputs_pl_kernel(
             for g in range(3):
                 first_layer(c, g)
 
+        def keep_warm():
+            nc.tensor.matmul_mx(
+                out=p_ps[3][:].rearrange("p j t -> p (j t)"),
+                lhsT=w_words[0][:, 0:P].bitcast(FP8X4),
+                lhsT_scale=w_plane[0][:, 0:P],
+                rhs=x_words[0].bitcast(FP4X4),
+                rhs_scale=x_plane[0],
+                start=True,
+                stop=True,
+            )
+
+        keep_warm()
+        keep_warm()
+
         def copy_z(c, lo=0, hi=CHUNK):
             first = HALO + WIDE * c
             nc.scalar.copy(
@@ -147,8 +161,8 @@ def tile_mix_momentum_of_two_inputs_pl_kernel(
 
         copy_z(0, 0, CHUNK // 2)
         copy_z(0, CHUNK // 2, CHUNK)
-        for c in range(1, CHUNKS):
-            copy_z(c)
+        copy_z(1)
+        copy_z(2)
 
         def z_back(c, back, lo, hi):
             first = HALO + WIDE * c - PACK * back
@@ -208,18 +222,28 @@ def tile_mix_momentum_of_two_inputs_pl_kernel(
             cols = slice(CHUNK * first, CHUNK * last)
             nc.sync.dma_start(out=out_1[0].rearrange("p c t -> p (c t)").bitcast(I32)[:, cols], in_=y_words[:, cols])
 
+        def round_from_psum(c, bank):
+            nc.vector.tensor_tensor(
+                out=y_bf[c][:].rearrange("p (t i) -> p t i", i=PACK),
+                in0=bank[:].rearrange("p i t -> p t i"),
+                in1=bias[:].unsqueeze(1).to_broadcast([P, CHUNK, PACK]),
+                op=ALU.add,
+            )
+
         add_previous(0, 0, CHUNK // 2)
         add_previous(0, CHUNK // 2, CHUNK)
         add_second(0, 0, CHUNK // 2)
         add_second(0, CHUNK // 2, CHUNK)
         relu_scalar(0)
+        copy_z(3)
+        deal_plane(wb_plane, wb_plane_raw)
         add_previous(1)
         add_previous(2)
         add_second(1)
         relu_scalar(1)
-        deal_plane(wb_plane, wb_plane_raw)
         quantise_hid(0)
         second_layer(0, p_ps[0])
+        keep_warm()
         add_second(2)
         relu_scalar(2)
         store_y(0)
@@ -230,27 +254,23 @@ def tile_mix_momentum_of_two_inputs_pl_kernel(
         add_second(3)
         quantise_hid(2)
         second_layer(2, p_ps[2])
+        second_layer(2, z_ps[0])
         store_y(2)
         relu_vector(3)
         round_y(0)
         quantise_hid(3)
-        second_layer(3, z_ps[0])
+        second_layer(3, z_ps[1])
         second_layer(3, p_ps[3])
         store_y(3)
         quantise_y(0)
         round_y(1)
-        round_y(2)
+        round_from_psum(2, z_ps[0])
         quantise_y(1)
-        nc.vector.tensor_tensor(
-            out=y_bf[3][:].rearrange("p (t i) -> p t i", i=PACK),
-            in0=z_ps[0][:].rearrange("p i t -> p t i"),
-            in1=bias[:].unsqueeze(1).to_broadcast([P, CHUNK, PACK]),
-            op=ALU.add,
-        )
+        store_words(0, 2)
+        round_from_psum(3, z_ps[1])
         quantise_y(2)
-        store_words(0, 3)
         quantise_y(3)
-        store_words(3, 4)
+        store_words(2, 4)
         for q in range(4):
             queue = nc.sync if q % 2 else nc.scalar
             queue.dma_start(

from contextlib import ExitStack

import concourse.mybir as mybir

K, L, T, R, N = 1024, 512, 512, 512, 512
FLOPS = 2 * (K + L) * R * T + 2 * R * N * T

F32 = mybir.dt.float32
BF16 = mybir.dt.bfloat16
I32 = mybir.dt.int32
U8 = mybir.dt.uint8
FP8X4 = mybir.dt.float8_e4m3fn_x4
FP4X4 = mybir.dt.float4_e2m1fn_x4
ALU = mybir.AluOpType
ACT = mybir.ActivationFunctionType

P = 128
PACK = 4
CHUNK = 128
CHUNKS = T // CHUNK
WIDE = CHUNK * PACK
HALO = 2 * PACK


def tile_mix_momentum_of_two_inputs_pl_kernel(
    tc, xt_words, xt_scales, wa_words, wa_scales, xq_words, xq_scales, wc_words, wc_scales, wb_words, wb_scales, b,
    out_0, out_1, out_2,
):
    nc = tc.nc
    with ExitStack() as ctx:
        sb = ctx.enter_context(tc.tile_pool(name="sb", bufs=1))
        ps = ctx.enter_context(tc.psum_pool(name="ps", bufs=1))
        ctx.enter_context(tc.manual_schedule())

        def tiles(pool, name, count, shape, dtype):
            return [pool.tile(shape, dtype, name="%s%d" % (name, i), align_bytes=64) for i in range(count)]

        xt_sb = sb.tile([P, 2, 2 * T], U8, align_bytes=64)
        xq_sb = sb.tile([P, 2 * T], U8, align_bytes=64)
        wa_raw = sb.tile([P, 2, R], I32, align_bytes=64)
        wc_raw = sb.tile([P, R], I32, align_bytes=64)
        planes = sb.tile([P, 7 * T], U8, align_bytes=64)
        x_words = [xt_sb[:, 0, :], xt_sb[:, 1, :], xq_sb[:]]
        w_raw = [wa_raw[:, 0, :], wa_raw[:, 1, :], wc_raw[:]]
        w_plane_raw = [planes[:, 0:T], planes[:, T : 2 * T], planes[:, 4 * T : 5 * T]]
        x_plane = [planes[:, 2 * T : 3 * T], planes[:, 3 * T : 4 * T], planes[:, 5 * T : 6 * T]]
        wb_plane_raw = planes[:, 6 * T : 7 * T]
        w_words = tiles(sb, "w_words", 3, [P, R], I32)
        w_plane = tiles(sb, "w_plane", 3, [P, R], U8)
        wb_raw = sb.tile([P, 2 * N], U8, align_bytes=64)
        wb_dealt = sb.tile([P, 2 * N], U8, align_bytes=64)
        wb_plane = sb.tile([P, N], U8, align_bytes=64)
        bias = sb.tile([P, PACK], F32, align_bytes=64)
        warm = sb.tile([P, 1], F32, align_bytes=64)
        z = sb.tile([P, HALO + PACK * T], F32, align_bytes=64)
        part = tiles(sb, "part", CHUNKS, [P, WIDE], F32)
        pre = tiles(sb, "pre", CHUNKS, [P, WIDE], BF16)
        hid = tiles(sb, "hid", CHUNKS, [P, WIDE], BF16)
        hid_words = tiles(sb, "hid_words", CHUNKS, [P, CHUNK], I32)
        hid_plane = tiles(sb, "hid_plane", CHUNKS, [P, CHUNK], U8)
        y = tiles(sb, "y", CHUNKS, [P, PACK, CHUNK], F32)
        y_bf = tiles(sb, "y_bf", CHUNKS, [P, WIDE], BF16)
        y_words = sb.tile([P, T], I32, align_bytes=64)
        y_plane = sb.tile([P, T], U8, align_bytes=64)
        z_ps = [ps.tile([P, PACK, CHUNK], F32, name="z_ps%d" % c) for c in range(CHUNKS)]
        p_ps = [ps.tile([P, PACK, CHUNK], F32, name="p_ps%d" % c) for c in range(CHUNKS)]

        def load_scales(queue, first, scales, q):
            passes = scales.shape[0]
            dst = planes[32 * q : 32 * q + 4, T * first : T * (first + passes)].bitcast(I32)
            queue.dma_start(
                out=dst.rearrange("r (g c) -> r g c", g=passes),
                in_=scales[:, 4 * q : 4 * q + 4, :].bitcast(I32).rearrange("g r c -> r g c"),
            )

        nc.vector.memset(planes[:, 0 : 2 * T].bitcast(I32), 0)
        nc.vector.memset(planes[:, 2 * T : 7 * T].bitcast(I32), 0)
        nc.vector.memset(z[:, 0:HALO], 0.0)
        nc.scalar.activation(out=warm[:], in_=z[:, 0:1], func=ACT.Identity)

        for q in range(2):
            load_scales(nc.gpsimd, 5, xq_scales, q)
        nc.sync.dma_start(out=xt_sb[:].bitcast(I32), in_=xt_words.bitcast(I32).rearrange("g p c -> p g c"))
        for q in range(4):
            load_scales(nc.sync, 0, wa_scales, q)
        nc.sync.dma_start(out=wa_raw[:], in_=wa_words.rearrange("g p c t -> p g (c t)").bitcast(I32))
        for q in range(4):
            load_scales(nc.sync, 2, xt_scales, q)
        nc.sync.dma_start(out=wc_raw[:], in_=wc_words[0].rearrange("p c t -> p (c t)").bitcast(I32))
        nc.sync.dma_start(out=xq_sb[:].bitcast(I32), in_=xq_words[0].bitcast(I32))
        for q in range(4):
            load_scales(nc.sync, 4, wc_scales, q)
        for q in range(2, 4):
            load_scales(nc.sync, 5, xq_scales, q)
        nc.sync.dma_start(out=wb_raw[:].bitcast(I32), in_=wb_words[0].bitcast(I32))
        for q in range(4):
            load_scales(nc.sync, 6, wb_scales, q)
        nc.sync.dma_start(out=bias[:], in_=b.rearrange("(p i) o -> p (i o)", i=PACK))

        def deal_plane(dst, src):
            nc.vector.tensor_copy(
                out=dst[:].rearrange("p (j h l) -> p h j l", j=PACK, l=16),
                in_=src.rearrange("p (h l j) -> p h j l", j=PACK, l=16),
            )

        def deal_words(g):
            nc.vector.tensor_copy(
                out=w_words[g][:].rearrange("p (j h l) -> p h j l", j=PACK, l=4),
                in_=w_raw[g].rearrange("p (h l j) -> p h j l", j=PACK, l=4),
            )

        deal_plane(w_plane[0], w_plane_raw[0])
        deal_plane(w_plane[1], w_plane_raw[1])
        deal_words(0)
        deal_words(1)
        deal_words(2)
        deal_plane(w_plane[2], w_plane_raw[2])
        nc.vector.tensor_copy(
            out=wb_dealt[:].rearrange("p (j h l e) -> p h j l e", j=PACK, l=8, e=2),
            in_=wb_raw[:].rearrange("p (h l j e) -> p h j l e", j=PACK, l=8, e=2),
        )

        def first_layer(c, g):
            for j in range(PACK):
                nc.tensor.matmul_mx(
                    out=z_ps[c][:, j, :],
                    lhsT=w_words[g][:, P * j : P * (j + 1)].bitcast(FP8X4),
                    lhsT_scale=w_plane[g][:, P * j : P * (j + 1)],
                    rhs=x_words[g][:, 2 * CHUNK * c : 2 * CHUNK * (c + 1)].bitcast(FP4X4),
                    rhs_scale=x_plane[g][:, CHUNK * c : CHUNK * (c + 1)],
                    start=(g == 0 and j == 0),
                    stop=(g == 2 and j == PACK - 1),
                )

        for c, g in [(0, 0), (0, 1), (1, 0), (0, 2), (1, 1), (1, 2)]:
            first_layer(c, g)
        for c in range(2, CHUNKS):
            for g in range(3):
                first_layer(c, g)

        def keep_warm():
            nc.tensor.matmul_mx(
                out=p_ps[3][:].rearrange("p j t -> p (j t)"),
                lhsT=w_words[0][:, 0:P].bitcast(FP8X4),
                lhsT_scale=w_plane[0][:, 0:P],
                rhs=x_words[0].bitcast(FP4X4),
                rhs_scale=x_plane[0],
                start=True,
                stop=True,
            )

        keep_warm()
        keep_warm()

        def copy_z(c, lo=0, hi=CHUNK):
            first = HALO + WIDE * c
            nc.scalar.copy(
                out=z[:, first + PACK * lo : first + PACK * hi].rearrange("p (t j) -> p t j", j=PACK),
                in_=z_ps[c][:, :, lo:hi].rearrange("p j t -> p t j"),
            )

        copy_z(0, 0, CHUNK // 2)
        copy_z(0, CHUNK // 2, CHUNK)
        copy_z(1)
        copy_z(2)

        def z_back(c, back, lo, hi):
            first = HALO + WIDE * c - PACK * back
            return z[:, first + PACK * lo : first + PACK * hi]

        def add_previous(c, lo=0, hi=CHUNK):
            nc.vector.scalar_tensor_tensor(
                out=part[c][:, PACK * lo : PACK * hi], in0=z_back(c, 1, lo, hi), scalar=0.5, in1=z_back(c, 0, lo, hi),
                op0=ALU.mult, op1=ALU.add,
            )

        def add_second(c, lo=0, hi=CHUNK):
            nc.vector.scalar_tensor_tensor(
                out=pre[c][:, PACK * lo : PACK * hi], in0=z_back(c, 2, lo, hi), scalar=0.25,
                in1=part[c][:, PACK * lo : PACK * hi], op0=ALU.mult, op1=ALU.add,
            )

        def relu_scalar(c):
            nc.scalar.activation(out=hid[c][:], in_=pre[c][:], func=ACT.Relu)

        def relu_vector(c):
            nc.vector.tensor_scalar_max(out=hid[c][:], in0=pre[c][:], scalar1=0.0)

        def quantise_hid(c):
            nc.vector.quantize_mx(out=hid_words[c][:].bitcast(FP8X4), scales=hid_plane[c][:], in_=hid[c][:])

        def second_layer(c, bank):
            for i in range(PACK):
                nc.tensor.matmul_mx(
                    out=bank[:, i, :],
                    lhsT=wb_dealt[:, 2 * P * i : 2 * P * (i + 1)].bitcast(FP4X4),
                    lhsT_scale=wb_plane[:, P * i : P * (i + 1)],
                    rhs=hid_words[c][:].bitcast(FP8X4),
                    rhs_scale=hid_plane[c][:],
                    start=True,
                    stop=True,
                )

        def store_y(c):
            for i in range(PACK):
                nc.scalar.activation(out=y[c][:, i, :], in_=p_ps[c][:, i, :], func=ACT.Identity, bias=bias[:, i : i + 1])
            nc.sync.dma_start(
                out=out_0.rearrange("(p i) t -> p i t", i=PACK)[:, :, CHUNK * c : CHUNK * (c + 1)], in_=y[c][:]
            )

        def round_y(c):
            nc.vector.tensor_copy(
                out=y_bf[c][:].rearrange("p (h l i) -> p h i l", i=PACK, l=4),
                in_=y[c][:].rearrange("p i (h l) -> p h i l", l=4),
            )

        def quantise_y(c):
            cols = slice(CHUNK * c, CHUNK * (c + 1))
            nc.vector.quantize_mx(out=y_words[:, cols].bitcast(FP8X4), scales=y_plane[:, cols], in_=y_bf[c][:])

        def store_words(first, last):
            cols = slice(CHUNK * first, CHUNK * last)
            nc.sync.dma_start(out=out_1[0].rearrange("p c t -> p (c t)").bitcast(I32)[:, cols], in_=y_words[:, cols])

        def round_from_psum(c, bank):
            nc.vector.tensor_tensor(
                out=y_bf[c][:].rearrange("p (t i) -> p t i", i=PACK),
                in0=bank[:].rearrange("p i t -> p t i"),
                in1=bias[:].unsqueeze(1).to_broadcast([P, CHUNK, PACK]),
                op=ALU.add,
            )

        add_previous(0, 0, CHUNK // 2)
        add_previous(0, CHUNK // 2, CHUNK)
        add_second(0, 0, CHUNK // 2)
        add_second(0, CHUNK // 2, CHUNK)
        relu_scalar(0)
        copy_z(3)
        deal_plane(wb_plane, wb_plane_raw)
        add_previous(1)
        add_previous(2)
        add_second(1)
        relu_scalar(1)
        quantise_hid(0)
        second_layer(0, p_ps[0])
        keep_warm()
        add_second(2)
        relu_scalar(2)
        store_y(0)
        add_previous(3)
        quantise_hid(1)
        second_layer(1, p_ps[1])
        store_y(1)
        add_second(3)
        quantise_hid(2)
        second_layer(2, p_ps[2])
        second_layer(2, z_ps[0])
        store_y(2)
        relu_vector(3)
        round_y(0)
        quantise_hid(3)
        second_layer(3, z_ps[1])
        second_layer(3, p_ps[3])
        store_y(3)
        quantise_y(0)
        round_y(1)
        round_from_psum(2, z_ps[0])
        quantise_y(1)
        store_words(0, 2)
        round_from_psum(3, z_ps[1])
        quantise_y(2)
        quantise_y(3)
        store_words(2, 4)
        for q in range(4):
            queue = nc.sync if q % 2 else nc.scalar
            queue.dma_start(
                out=out_2[0, 4 * q : 4 * q + 4, :].bitcast(I32), in_=y_plane[32 * q : 32 * q + 4, :].bitcast(I32)
            )
